import numpy as np
import ml_dtypes


def mxq(x, axis, fmt="e4m3"):
    dtype, down = {"e4m3": (ml_dtypes.float8_e4m3fn, 7), "e5m2": (ml_dtypes.float8_e5m2, 14)}[fmt]
    v = np.moveaxis(np.asarray(x, np.float32).astype(ml_dtypes.bfloat16).astype(np.float64), axis, -1)
    blocks = v.reshape(v.shape[:-1] + (-1, 32))
    amax = np.abs(blocks).max(-1, keepdims=True)
    byte = np.maximum(np.where(amax > 0, np.frexp(amax)[1] - 1 + 127, 0) - down, 1)
    scale = np.exp2(byte - 127.0)
    codes = (blocks / scale).astype(np.float32).astype(dtype).astype(np.float64)
    return np.moveaxis((codes * scale).reshape(v.shape), -1, axis)


WIDE = False


def mx_kscale(k):
    if not WIDE:
        return np.ones(k)
    levels = np.array([10, -10, 5, -5, 0])
    if k % 512:
        return np.exp2(np.random.permutation(np.resize(levels, k // 32))).repeat(32)
    a = np.empty((k // 512, 16))
    for p in range(k // 512):
        a[p, :8] = np.random.permutation(np.resize(levels, 8))
        for g in range(8):
            far = levels[np.abs(levels - a[p, g]) >= 10]
            a[p, g + 8] = far[np.random.randint(len(far))]
    return np.exp2(a.ravel()).repeat(32)


def f64(x):
    return np.asarray(x).astype(np.float64)


def striped(idx):
    return np.tile(idx.reshape(-1, 16).T, (8, 1)).astype(np.uint16)


def unstriped(offs):
    return offs[:16].T.reshape(-1).astype(np.int64)


def striped8(idx):
    return np.concatenate([x.reshape(-1, 16).T for x in idx]).astype(np.uint16)


def runs(offs, k):
    lists = np.stack([offs[16 * r : 16 * r + 16].T.reshape(-1) for r in range(8)]).astype(np.int64)
    return lists[np.arange(k) % 512 // 64]


def pack_weight(w):
    k, n = w.shape
    w = f64(np.asarray(w, np.float32).astype(ml_dtypes.bfloat16)).reshape(k // 32, 32, n)
    amax = np.abs(w).max(1)
    byte = np.clip(np.where(amax > 0, np.frexp(amax)[1] - 1 + 127 - 7, 1), 1, 254)
    scaled = (w * np.exp2(127.0 - byte)[:, None, :]).reshape(k, n).astype(np.float32)
    words = np.ascontiguousarray(scaled.reshape(k // 512, 128, 4, n).transpose(0, 1, 3, 2)).astype(ml_dtypes.float8_e4m3fn).view(np.uint8)
    return words, np.ascontiguousarray(byte.astype(np.uint8).reshape(k // 512, 16, n))


def unpack_weight(words, scales):
    g, p, n, _ = words.shape
    vals = np.ascontiguousarray(words).view(ml_dtypes.float8_e4m3fn).astype(np.float64) * np.repeat(np.exp2(scales.astype(np.float64) - 127.0), 8, axis=1)[..., None]
    return vals.transpose(0, 1, 3, 2).reshape(g * 512, n)


K, T, S, V, H, W, G = 512, 2048, 512, 512, 512, 384, 2048


def setup_inputs():
    n = np.random.standard_normal
    s = mx_kscale(K)[:, None]
    u = mx_kscale(S)
    packed_xT = pack_weight(n((K, T)) * s)
    return {
        "x_words": packed_xT[0],
        "x_scales": packed_xT[1],
        "w1": (n((K, H)) / np.sqrt(K) / s).astype(np.float32),
        "w2": (n((K, H)) / np.sqrt(K) / s).astype(np.float32),
        "ga": (np.random.uniform(0.5, 1.5, (H, 1)) * u[:, None]).astype(np.float32),
        "gb": (np.random.uniform(0.5, 1.5, (H, 1)) / u[:, None]).astype(np.float32),
        "offs": striped8(np.random.randint(0, T, (8, S))),
        "two": striped(np.random.permutation(T)[:V]),
        "n1": striped(np.random.permutation(S)[:W]),
        "n2": striped(np.random.permutation(S)[:W]),
        "n3": striped8(np.stack([np.random.permutation(V) for _ in range(8)])),
        "n4": striped8(np.stack([np.random.permutation(V) for _ in range(8)])),
        "n5": striped(np.random.randint(0, V, G)),
    }


def reference(x_words, x_scales, w1, w2, ga, gb, offs, two, n1, n2, n3, n4, n5):
    xq = unpack_weight(x_words, x_scales)[np.arange(K)[:, None], runs(offs, K)]
    a = mxq(f64(w1), 0, "e4m3").T @ xq
    old = a[:, unstriped(n1)]
    pa = a[:, unstriped(n2)]
    ra = old - np.tanh(pa)
    ds = a.copy()
    ds[:, unstriped(n1)] = ra
    z = f64(ga) * ds
    x_two = unpack_weight(x_words, x_scales)[:, unstriped(two)]
    b = mxq(f64(w2), 0, "e4m3").T @ x_two
    z2 = f64(gb) * ((b[np.arange(H)[:, None], runs(n3, H)]) * (b[np.arange(H)[:, None], runs(n4, H)]))
    s = 0.0625 * ((mxq(z, 0, "e4m3").T @ mxq(z2, 0, "e4m3")))
    mb = s[:, unstriped(n5)]
    mx = mb.reshape(S, V, 4).max(axis=2)
    return s - mx

@@ -1,0 +1,296 @@
+from contextlib import ExitStack
+
+import concourse.mybir as mybir
+
+F32 = mybir.dt.float32
+BF16 = mybir.dt.bfloat16
+I32 = mybir.dt.int32
+U32 = mybir.dt.uint32
+U16 = mybir.dt.uint16
+U8 = mybir.dt.uint8
+FP8X4 = mybir.dt.float8_e4m3fn_x4
+ALU = mybir.AluOpType
+ACT = mybir.ActivationFunctionType
+
+P = 128
+PACK = 4
+T = 2048
+N = 512
+W = 384
+G = 2048
+A_WIN = 768
+B_WIN = 1024
+S_WIN = 768
+CAST_SPLIT = 88
+V_COLS = 144
+S_COLS = 184
+
+FLOPS = 3 * 2 * 512 * 512 * 512
+
+
+def tile_picked_hkqktanhprodgmaxd_none_p_kernel(
+    tc, x_words, x_scales, w1, w2, ga, gb, offs, two, n1, n2, n3, n4, n5, out
+):
+    nc = tc.nc
+    with ExitStack() as ctx:
+        lists = ctx.enter_context(tc.tile_pool(name="lists", bufs=1))
+        keep = ctx.enter_context(tc.tile_pool(name="keep", bufs=1))
+        psum = ctx.enter_context(tc.psum_pool(name="psum", bufs=1))
+
+        def sb(name, shape, dtype):
+            return keep.tile(shape, dtype, name=name, align_bytes=64)
+
+        def load_list(name, src):
+            tile = lists.tile(list(src.shape), U16, name=name)
+            nc.sync.dma_start(tile[:], src)
+            return tile
+
+        xs = sb("xs", [P, T], U8)
+        a_win = [sb("a_win%d" % t, [P, A_WIN], F32) for t in range(PACK)]
+        b_win = [sb("b_win%d" % t, [P, B_WIN], F32) for t in range(PACK)]
+        s_win = [sb("s_win%d" % t, [P, S_WIN], F32) for t in range(PACK)]
+        minus_half = sb("minus_half", [P, W], F32)
+        for win in a_win + b_win + s_win:
+            nc.vector.memset(win[:, N:], 0.0)
+        nc.vector.memset(minus_half[:], -0.5)
+
+        rows = x_scales[0].bitcast(I32).rearrange("(g e) c -> e g c", e=2)
+        xs_i = xs[:].bitcast(I32)
+        for r in range(2):
+            nc.sync.dma_start(xs_i[r:P:2, :], rows[r].unsqueeze(1).to_broadcast([8, 8, T // 4]))
+        offs_t = load_list("offs_t", offs)
+        two_t = load_list("two_t", two)
+        n2_t = load_list("n2_t", n2)
+        n1_t = load_list("n1_t", n1)
+        xw = sb("xw", [P, T], I32)
+        nc.sync.dma_start(xw[:], x_words[0].rearrange("p n t -> p (n t)").bitcast(I32))
+        w1_raw = sb("w1_raw", [P, PACK, N], F32)
+        nc.sync.dma_start(w1_raw[:], w1.rearrange("(p j) c -> p j c", j=PACK))
+        w2_raw = sb("w2_raw", [P, PACK, N], F32)
+        nc.sync.dma_start(w2_raw[:], w2.rearrange("(p j) c -> p j c", j=PACK))
+        n3_t = load_list("n3_t", n3)
+        n4_t = load_list("n4_t", n4)
+        ga_t = sb("ga_t", [P, PACK], F32)
+        gb_t = sb("gb_t", [P, PACK], F32)
+        nc.gpsimd.dma_start(ga_t[:], ga.rearrange("(p t) o -> p (t o)", t=PACK))
+        nc.gpsimd.dma_start(gb_t[:], gb.rearrange("(p t) o -> p (t o)", t=PACK))
+        n5_t = load_list("n5_t", n5)
+
+        xa_words = sb("xa_words", [P, N], U32)
+        xb_words = sb("xb_words", [P, N], U32)
+
+        def pick_scales(name, picks):
+            picked = sb(name + "_bytes", [P, N], U8)
+            plane = sb(name + "_scales", [P, N], U8)
+            nc.vector.tensor_copy(picked[:], xs[:].indirect(picks[:]))
+            nc.vector.tensor_copy(plane[:].bitcast(I32), picked[:].bitcast(I32))
+            for r in range(2):
+                nc.scalar.dma_start(plane[:].bitcast(I32)[2 + r : P : 32, :], picked[:].bitcast(I32)[16 + r : P : 32, :])
+            return plane
+
+        xa_scales = pick_scales("xa", offs_t)
+        xb_scales = pick_scales("xb", two_t)
+        nc.vector.tensor_copy(xa_words[:], xw[:].bitcast(U32).indirect(offs_t[:]))
+        nc.vector.tensor_copy(xb_words[:], xw[:].bitcast(U32).indirect(two_t[:]))
+
+        def cast_views(raw, grouped, lo, hi):
+            src = raw[:].rearrange("p j (m t) -> p m j t", t=PACK)[:, lo:hi]
+            dst = grouped[:].rearrange("p (t m j) -> p m j t", t=PACK, j=PACK)[:, lo:hi]
+            return dst, src
+
+        def quantize(codes, scales, grouped, lo, hi):
+            nc.vector.quantize_mx(
+                out=codes[:, lo:hi].bitcast(FP8X4), scales=scales[:, lo:hi], in_=grouped[:, PACK * lo : PACK * hi]
+            )
+
+        def product(bank, l_codes, l_scales, blk, r_codes, r_scales):
+            cols = slice(blk * P, (blk + 1) * P)
+            nc.tensor.matmul_mx(
+                out=bank[:],
+                lhsT=l_codes[:, cols].bitcast(FP8X4),
+                lhsT_scale=l_scales[:, cols],
+                rhs=r_codes[:].bitcast(FP8X4),
+                rhs_scale=r_scales[:],
+                start=True,
+                stop=True,
+            )
+
+        w1_g = sb("w1_g", [P, PACK * N], BF16)
+        w1_codes = sb("w1_codes", [P, N], U32)
+        w1_scales = sb("w1_scales", [P, N], U8)
+        nc.vector.tensor_copy(*cast_views(w1_raw, w1_g, 0, CAST_SPLIT))
+        nc.scalar.copy(*cast_views(w1_raw, w1_g, CAST_SPLIT, P))
+        a_bank = [psum.tile([P, N], F32, name="a_bank%d" % t, tag="bank%d" % t) for t in range(PACK)]
+        for t in range(PACK):
+            quantize(w1_codes, w1_scales, w1_g, t * P, (t + 1) * P)
+            product(a_bank[t], w1_codes, w1_scales, t, xa_words, xa_scales)
+
+        w2_g = sb("w2_g", [P, PACK * N], BF16)
+        w2_codes = sb("w2_codes", [P, N], U32)
+        w2_scales = sb("w2_scales", [P, N], U8)
+        b_bank = [psum.tile([P, N], F32, name="b_bank%d" % t, tag="bank%d" % (PACK + t)) for t in range(PACK)]
+
+        sig = [sb("sig%d" % t, [P, W], F32) for t in range(PACK)]
+        upd = [sb("upd%d" % t, [P, W], F32) for t in range(PACK)]
+
+        def a_front(t):
+            nc.scalar.activation(a_win[t][:, :N], a_bank[t][:], ACT.Copy, scale=0.5)
+            nc.scalar.activation(sig[t][:], a_win[t][:].indirect(n2_t[:]), ACT.Sigmoid, scale=-4.0)
+
+        def a_add(t):
+            nc.vector.tensor_tensor(upd[t][:], a_win[t][:].indirect(n1_t[:]), sig[t][:], ALU.add)
+
+        def a_put_scalar(t):
+            nc.scalar.activation(a_win[t][:].indirect(n1_t[:]), upd[t][:], ACT.Copy, bias=-0.5)
+
+        def a_put_vector(t):
+            nc.vector.tensor_tensor(a_win[t][:].indirect(n1_t[:]), upd[t][:], minus_half[:], ALU.add)
+
+        z_planes = sb("z_planes", [P, PACK, N], BF16)
+        z2_planes = sb("z2_planes", [P, PACK, N], BF16)
+        ga2 = sb("ga2", [P, PACK], F32)
+
+        def z_scale_vector(t):
+            nc.vector.tensor_scalar(z_planes[:, t, :], a_win[t][:, :N], ga2[:, t : t + 1], None, ALU.mult)
+
+        def z_scale_scalar(t):
+            nc.scalar.activation(z_planes[:, t, :], a_win[t][:, :N], ACT.Copy, scale=ga2[:, t : t + 1])
+
+        b3 = [sb("b3_%d" % t, [P, N], F32) for t in range(PACK)]
+        prod = [sb("prod%d" % t, [P, N], F32) for t in range(PACK)]
+
+        def b_times(t):
+            nc.vector.tensor_tensor(prod[t][:], b_win[t][:].indirect(n4_t[:]), b3[t][:], ALU.mult)
+
+        def z2_scale(t):
+            nc.vector.tensor_scalar(z2_planes[:, t, :], prod[t][:], gb_t[:, t : t + 1], None, ALU.mult)
+
+        def weave_views(grouped, planes, lo, hi):
+            src = planes[:, :, lo:hi].rearrange("p t (c i) -> p c t i", i=4)
+            dst = grouped[:, PACK * lo : PACK * hi].rearrange("p (c i t) -> p c t i", i=4, t=PACK)
+            return dst, src
+
+        a_front(0)
+        nc.vector.tensor_copy(*cast_views(w2_raw, w2_g, 0, P))
+        a_add(0)
+        a_front(1)
+        quantize(w2_codes, w2_scales, w2_g, 0, N)
+        for t in range(PACK):
+            product(b_bank[t], w2_codes, w2_scales, t, xb_words, xb_scales)
+        nc.vector.tensor_scalar(ga2[:], ga_t[:], 2.0, None, ALU.mult)
+        a_add(1)
+        a_front(2)
+        nc.vector.tensor_copy(b_win[0][:, :N], b_bank[0][:])
+        a_add(2)
+        a_front(3)
+        nc.vector.tensor_copy(b3[0][:], b_win[0][:].indirect(n3_t[:]))
+        a_add(3)
+        for t in range(1, PACK):
+            nc.scalar.copy(b_win[t][:, :N], b_bank[t][:])
+        b_times(0)
+        a_put_vector(3)
+        z2_scale(0)
+        for t in range(1, PACK):
+            nc.scalar.activation(b3[t][:], b_win[t][:].indirect(n3_t[:]), ACT.Copy)
+            a_put_scalar(t - 1)
+        b_times(1)
+        z_scale_vector(3)
+        z2_scale(1)
+        b_times(2)
+        z_scale_vector(0)
+        z2_scale(2)
+        b_times(3)
+        z_scale_vector(1)
+        z2_scale(3)
+        z_scale_scalar(2)
+
+        z2_g = sb("z2_g", [P, PACK * N], BF16)
+        z2_codes = sb("z2_codes", [P, N], U32)
+        z2_scales = sb("z2_scales", [P, N], U8)
+        z_g = [sb("z_g%d" % i, [P, N], BF16) for i in range(PACK)]
+        z_codes = sb("z_codes", [P, N], U32)
+        z_scales = sb("z_scales", [P, N], U8)
+        half = N // 2
+        for h in range(2):
+            nc.vector.tensor_copy(*weave_views(z2_g, z2_planes, h * half, (h + 1) * half))
+        for h in range(2):
+            quantize(z2_codes, z2_scales, z2_g, h * half, (h + 1) * half)
+
+        def z_weave(i, copy):
+            src = z_planes[:, :, i * P : (i + 1) * P].rearrange("p t (c i) -> p c t i", i=4)
+            dst = z_g[i][:].rearrange("p (c i t) -> p c t i", i=4, t=PACK)
+            copy(dst, src)
+
+        def z_quantize(i):
+            cols = slice(i * P, (i + 1) * P)
+            nc.vector.quantize_mx(out=z_codes[:, cols].bitcast(FP8X4), scales=z_scales[:, cols], in_=z_g[i][:])
+
+        z_weave(0, nc.vector.tensor_copy)
+        z_weave(1, nc.vector.tensor_copy)
+        z_weave(2, nc.scalar.copy)
+        z_weave(3, nc.scalar.copy)
+        s_bank = [psum.tile([P, N], F32, name="s_bank%d" % i, tag="bank%d" % i) for i in range(PACK)]
+        for i in range(PACK):
+            z_quantize(i)
+            product(s_bank[i], z_codes, z_scales, i, z2_codes, z2_scales)
+
+        mb = [sb("mb%d" % i, [P, G], F32) for i in range(PACK)]
+        pair = [sb("pair%d" % i, [P, G // 2], F32) for i in range(PACK)]
+        top = [sb("top%d" % i, [P, N], F32) for i in range(PACK)]
+        res = [sb("res%d" % i, [P, N], F32) for i in range(PACK)]
+
+        def s_out(i):
+            nc.scalar.activation(s_win[i][:, :N], s_bank[i][:], ACT.Copy, scale=0.0625)
+
+        def members(i, lo, hi):
+            return mb[i][:, 4 * lo : 4 * hi], s_win[i][:].indirect(n5_t[:, lo // 4 : hi // 4])
+
+        def fetch_scalar(i):
+            for k in range(2):
+                lo = V_COLS + k * S_COLS
+                dst, src = members(i, lo, lo + S_COLS)
+                nc.scalar.activation(dst, src, ACT.Copy)
+
+        def fetch_vector(i, k):
+            nc.vector.tensor_copy(*members(i, k * V_COLS // 2, (k + 1) * V_COLS // 2))
+
+        def max_pairs(i, lo, hi):
+            four = mb[i][:, 4 * lo : 4 * hi].rearrange("p (v a b) -> p v a b", a=2, b=2)
+            two_ = pair[i][:, 2 * lo : 2 * hi].rearrange("p (v b) -> p v b", b=2)
+            nc.vector.tensor_tensor(two_, four[:, :, 0, :], four[:, :, 1, :], ALU.max)
+
+        def max_top(i, lo, hi):
+            two_ = pair[i][:, 2 * lo : 2 * hi].rearrange("p (v b) -> p v b", b=2)
+            nc.vector.tensor_tensor(top[i][:, lo:hi], two_[:, :, 0], two_[:, :, 1], ALU.max)
+
+        def finish(i, lo, hi):
+            nc.vector.tensor_tensor(res[i][:, lo:hi], s_win[i][:, lo:hi], top[i][:, lo:hi], ALU.subtract)
+            nc.sync.dma_start(out[i * P : (i + 1) * P, lo:hi], res[i][:, lo:hi])
+
+        s_out(0)
+        for i in range(PACK):
+            if i + 1 < PACK:
+                s_out(i + 1)
+            fetch_scalar(i)
+        for i in range(2):
+            fetch_vector(i, 0)
+            fetch_vector(i, 1)
+        for i in range(2):
+            max_pairs(i, 0, N)
+            fetch_vector(i + 2, 0)
+            max_top(i, 0, N)
+            fetch_vector(i + 2, 1)
+            finish(i, 0, N)
+        cuts = [0, V_COLS, V_COLS + S_COLS, N]
+        max_pairs(2, 0, N)
+        max_pairs(3, cuts[0], cuts[1])
+        max_top(2, 0, N)
+        max_top(3, cuts[0], cuts[1])
+        finish(2, 0, N)
+        max_pairs(3, cuts[1], cuts[2])
+        finish(3, cuts[0], cuts[1])
+        max_top(3, cuts[1], cuts[2])
+        max_pairs(3, cuts[2], cuts[3])
+        finish(3, cuts[1], cuts[2])
+        max_top(3, cuts[2], cuts[3])
+        finish(3, cuts[2], cuts[3])

@@ -16,14 +16,13 @@ P = 128
 PACK = 4
 T = 2048
 N = 512
+HALF = 256
 W = 384
 G = 2048
 A_WIN = 768
-B_WIN = 1024
 S_WIN = 768
-CAST_SPLIT = 88
 V_COLS = 144
-S_COLS = 184
+S_COLS = (N - V_COLS) // 2
 
 FLOPS = 3 * 2 * 512 * 512 * 512
 
@@ -45,19 +44,15 @@ def tile_picked_hkqktanhprodgmaxd_none_p_kernel(
             nc.sync.dma_start(tile[:], src)
             return tile
 
-        xs = sb("xs", [P, T], U8)
         a_win = [sb("a_win%d" % t, [P, A_WIN], F32) for t in range(PACK)]
-        b_win = [sb("b_win%d" % t, [P, B_WIN], F32) for t in range(PACK)]
         s_win = [sb("s_win%d" % t, [P, S_WIN], F32) for t in range(PACK)]
-        minus_half = sb("minus_half", [P, W], F32)
-        for win in a_win + b_win + s_win:
+        for win in a_win + s_win:
             nc.vector.memset(win[:, N:], 0.0)
-        nc.vector.memset(minus_half[:], -0.5)
 
+        xs = sb("xs", [P, T], U8)
         rows = x_scales[0].bitcast(I32).rearrange("(g e) c -> e g c", e=2)
-        xs_i = xs[:].bitcast(I32)
         for r in range(2):
-            nc.sync.dma_start(xs_i[r:P:2, :], rows[r].unsqueeze(1).to_broadcast([8, 8, T // 4]))
+            nc.sync.dma_start(xs[:].bitcast(I32)[r:P:2, :], rows[r].unsqueeze(1).to_broadcast([8, 8, T // 4]))
         offs_t = load_list("offs_t", offs)
         two_t = load_list("two_t", two)
         n2_t = load_list("n2_t", n2)
@@ -70,26 +65,26 @@ def tile_picked_hkqktanhprodgmaxd_none_p_kernel(
         nc.sync.dma_start(w2_raw[:], w2.rearrange("(p j) c -> p j c", j=PACK))
         n3_t = load_list("n3_t", n3)
         n4_t = load_list("n4_t", n4)
+        n5_t = load_list("n5_t", n5)
         ga_t = sb("ga_t", [P, PACK], F32)
         gb_t = sb("gb_t", [P, PACK], F32)
         nc.gpsimd.dma_start(ga_t[:], ga.rearrange("(p t) o -> p (t o)", t=PACK))
         nc.gpsimd.dma_start(gb_t[:], gb.rearrange("(p t) o -> p (t o)", t=PACK))
-        n5_t = load_list("n5_t", n5)
 
         xa_words = sb("xa_words", [P, N], U32)
         xb_words = sb("xb_words", [P, N], U32)
 
-        def pick_scales(name, picks):
+        def pick_scales(name, picks, queue):
             picked = sb(name + "_bytes", [P, N], U8)
             plane = sb(name + "_scales", [P, N], U8)
             nc.vector.tensor_copy(picked[:], xs[:].indirect(picks[:]))
             nc.vector.tensor_copy(plane[:].bitcast(I32), picked[:].bitcast(I32))
             for r in range(2):
-                nc.scalar.dma_start(plane[:].bitcast(I32)[2 + r : P : 32, :], picked[:].bitcast(I32)[16 + r : P : 32, :])
+                queue.dma_start(plane[:].bitcast(I32)[2 + r : P : 32, :], picked[:].bitcast(I32)[16 + r : P : 32, :])
             return plane
 
-        xa_scales = pick_scales("xa", offs_t)
-        xb_scales = pick_scales("xb", two_t)
+        xa_scales = pick_scales("xa", offs_t, nc.scalar)
+        xb_scales = pick_scales("xb", two_t, nc.sync)
         nc.vector.tensor_copy(xa_words[:], xw[:].bitcast(U32).indirect(offs_t[:]))
         nc.vector.tensor_copy(xb_words[:], xw[:].bitcast(U32).indirect(two_t[:]))
 
@@ -98,19 +93,17 @@ def tile_picked_hkqktanhprodgmaxd_none_p_kernel(
             dst = grouped[:].rearrange("p (t m j) -> p m j t", t=PACK, j=PACK)[:, lo:hi]
             return dst, src
 
-        def quantize(codes, scales, grouped, lo, hi):
-            nc.vector.quantize_mx(
-                out=codes[:, lo:hi].bitcast(FP8X4), scales=scales[:, lo:hi], in_=grouped[:, PACK * lo : PACK * hi]
-            )
+        def quantize(codes, scales, grouped):
+            nc.vector.quantize_mx(out=codes.bitcast(FP8X4), scales=scales, in_=grouped)
 
-        def product(bank, l_codes, l_scales, blk, r_codes, r_scales):
+        def product(acc, l_codes, l_scales, blk, r_codes, r_scales):
             cols = slice(blk * P, (blk + 1) * P)
             nc.tensor.matmul_mx(
-                out=bank[:],
+                out=acc,
                 lhsT=l_codes[:, cols].bitcast(FP8X4),
                 lhsT_scale=l_scales[:, cols],
-                rhs=r_codes[:].bitcast(FP8X4),
-                rhs_scale=r_scales[:],
+                rhs=r_codes.bitcast(FP8X4),
+                rhs_scale=r_scales,
                 start=True,
                 stop=True,
             )
@@ -118,179 +111,150 @@ def tile_picked_hkqktanhprodgmaxd_none_p_kernel(
         w1_g = sb("w1_g", [P, PACK * N], BF16)
         w1_codes = sb("w1_codes", [P, N], U32)
         w1_scales = sb("w1_scales", [P, N], U8)
-        nc.vector.tensor_copy(*cast_views(w1_raw, w1_g, 0, CAST_SPLIT))
-        nc.scalar.copy(*cast_views(w1_raw, w1_g, CAST_SPLIT, P))
+        nc.vector.tensor_copy(*cast_views(w1_raw, w1_g, 0, P))
         a_bank = [psum.tile([P, N], F32, name="a_bank%d" % t, tag="bank%d" % t) for t in range(PACK)]
         for t in range(PACK):
-            quantize(w1_codes, w1_scales, w1_g, t * P, (t + 1) * P)
-            product(a_bank[t], w1_codes, w1_scales, t, xa_words, xa_scales)
+            cols = slice(t * P, (t + 1) * P)
+            quantize(w1_codes[:, cols], w1_scales[:, cols], w1_g[:, t * N : (t + 1) * N])
+            product(a_bank[t][:], w1_codes, w1_scales, t, xa_words[:], xa_scales[:])
 
         w2_g = sb("w2_g", [P, PACK * N], BF16)
         w2_codes = sb("w2_codes", [P, N], U32)
         w2_scales = sb("w2_scales", [P, N], U8)
-        b_bank = [psum.tile([P, N], F32, name="b_bank%d" % t, tag="bank%d" % (PACK + t)) for t in range(PACK)]
-
-        sig = [sb("sig%d" % t, [P, W], F32) for t in range(PACK)]
-        upd = [sb("upd%d" % t, [P, W], F32) for t in range(PACK)]
-
-        def a_front(t):
-            nc.scalar.activation(a_win[t][:, :N], a_bank[t][:], ACT.Copy, scale=0.5)
-            nc.scalar.activation(sig[t][:], a_win[t][:].indirect(n2_t[:]), ACT.Sigmoid, scale=-4.0)
-
-        def a_add(t):
-            nc.vector.tensor_tensor(upd[t][:], a_win[t][:].indirect(n1_t[:]), sig[t][:], ALU.add)
-
-        def a_put_scalar(t):
-            nc.scalar.activation(a_win[t][:].indirect(n1_t[:]), upd[t][:], ACT.Copy, bias=-0.5)
-
-        def a_put_vector(t):
-            nc.vector.tensor_tensor(a_win[t][:].indirect(n1_t[:]), upd[t][:], minus_half[:], ALU.add)
-
-        z_planes = sb("z_planes", [P, PACK, N], BF16)
-        z2_planes = sb("z2_planes", [P, PACK, N], BF16)
         ga2 = sb("ga2", [P, PACK], F32)
+        b_bank = [psum.tile([P, N], F32, name="b_bank%d" % t, tag="bank%d" % (PACK + t)) for t in range(PACK)]
+        sig = [sb("sig%d" % t, [P, W], F32) for t in range(PACK)]
+        old = [sb("old%d" % t, [P, W], F32) for t in range(PACK)]
+        z_planes = sb("z_planes", [P, PACK, N], BF16)
 
-        def z_scale_vector(t):
+        def a_out(t):
+            nc.vector.tensor_scalar(a_win[t][:, :N], a_bank[t][:], 0.5, None, ALU.mult)
+
+        a_out(0)
+        a_out(1)
+        nc.vector.tensor_copy(*cast_views(w2_raw, w2_g, 0, P))
+        a_out(2)
+        quantize(w2_codes[:], w2_scales[:], w2_g[:])
+        for t in range(PACK):
+            product(b_bank[t][:], w2_codes, w2_scales, t, xb_words[:], xb_scales[:])
+        a_out(3)
+        nc.vector.tensor_scalar(ga2[:], ga_t[:], 2.0, None, ALU.mult)
+        for t in range(PACK):
+            nc.scalar.activation(sig[t][:], a_win[t][:].indirect(n2_t[:]), ACT.Sigmoid, scale=-4.0)
+            nc.scalar.activation(old[t][:], a_win[t][:].indirect(n1_t[:]), ACT.Copy, bias=-0.5)
+            nc.vector.tensor_tensor(a_win[t][:].indirect(n1_t[:]), old[t][:], sig[t][:], ALU.add)
+        for t in range(PACK):
             nc.vector.tensor_scalar(z_planes[:, t, :], a_win[t][:, :N], ga2[:, t : t + 1], None, ALU.mult)
 
-        def z_scale_scalar(t):
-            nc.scalar.activation(z_planes[:, t, :], a_win[t][:, :N], ACT.Copy, scale=ga2[:, t : t + 1])
+        def weave(grouped, planes):
+            nc.vector.tensor_copy(
+                grouped.rearrange("p (c i t) -> p c t i", i=4, t=PACK), planes.rearrange("p t (c i) -> p c t i", i=4)
+            )
 
-        b3 = [sb("b3_%d" % t, [P, N], F32) for t in range(PACK)]
-        prod = [sb("prod%d" % t, [P, N], F32) for t in range(PACK)]
-
-        def b_times(t):
-            nc.vector.tensor_tensor(prod[t][:], b_win[t][:].indirect(n4_t[:]), b3[t][:], ALU.mult)
-
-        def z2_scale(t):
-            nc.vector.tensor_scalar(z2_planes[:, t, :], prod[t][:], gb_t[:, t : t + 1], None, ALU.mult)
-
-        def weave_views(grouped, planes, lo, hi):
-            src = planes[:, :, lo:hi].rearrange("p t (c i) -> p c t i", i=4)
-            dst = grouped[:, PACK * lo : PACK * hi].rearrange("p (c i t) -> p c t i", i=4, t=PACK)
-            return dst, src
-
-        a_front(0)
-        nc.vector.tensor_copy(*cast_views(w2_raw, w2_g, 0, P))
-        a_add(0)
-        a_front(1)
-        quantize(w2_codes, w2_scales, w2_g, 0, N)
-        for t in range(PACK):
-            product(b_bank[t], w2_codes, w2_scales, t, xb_words, xb_scales)
-        nc.vector.tensor_scalar(ga2[:], ga_t[:], 2.0, None, ALU.mult)
-        a_add(1)
-        a_front(2)
-        nc.vector.tensor_copy(b_win[0][:, :N], b_bank[0][:])
-        a_add(2)
-        a_front(3)
-        nc.vector.tensor_copy(b3[0][:], b_win[0][:].indirect(n3_t[:]))
-        a_add(3)
-        for t in range(1, PACK):
-            nc.scalar.copy(b_win[t][:, :N], b_bank[t][:])
-        b_times(0)
-        a_put_vector(3)
-        z2_scale(0)
-        for t in range(1, PACK):
-            nc.scalar.activation(b3[t][:], b_win[t][:].indirect(n3_t[:]), ACT.Copy)
-            a_put_scalar(t - 1)
-        b_times(1)
-        z_scale_vector(3)
-        z2_scale(1)
-        b_times(2)
-        z_scale_vector(0)
-        z2_scale(2)
-        b_times(3)
-        z_scale_vector(1)
-        z2_scale(3)
-        z_scale_scalar(2)
-
-        z2_g = sb("z2_g", [P, PACK * N], BF16)
-        z2_codes = sb("z2_codes", [P, N], U32)
-        z2_scales = sb("z2_scales", [P, N], U8)
-        z_g = [sb("z_g%d" % i, [P, N], BF16) for i in range(PACK)]
+        z_g = sb("z_g", [P, PACK * N], BF16)
         z_codes = sb("z_codes", [P, N], U32)
         z_scales = sb("z_scales", [P, N], U8)
-        half = N // 2
-        for h in range(2):
-            nc.vector.tensor_copy(*weave_views(z2_g, z2_planes, h * half, (h + 1) * half))
-        for h in range(2):
-            quantize(z2_codes, z2_scales, z2_g, h * half, (h + 1) * half)
+        weave(z_g[:], z_planes[:])
 
-        def z_weave(i, copy):
-            src = z_planes[:, :, i * P : (i + 1) * P].rearrange("p t (c i) -> p c t i", i=4)
-            dst = z_g[i][:].rearrange("p (c i t) -> p c t i", i=4, t=PACK)
-            copy(dst, src)
+        b_win = [sb("b_win%d" % t, [P, N], F32) for t in range(PACK)]
+        for t in range(PACK):
+            nc.scalar.copy(b_win[t][:], b_bank[t][:])
+        z2_codes = sb("z2_codes", [P, N], U32)
+        z2_scales = sb("z2_scales", [P, N], U8)
+        z2_planes = [sb("z2_planes%d" % h, [P, PACK, HALF], BF16) for h in range(2)]
+        z2_g = [sb("z2_g%d" % h, [P, PACK * HALF], BF16) for h in range(2)]
+        left = [[sb("left%d_%d" % (h, t), [P, HALF], F32) for t in range(PACK)] for h in range(2)]
+        right = [[sb("right%d_%d" % (h, t), [P, HALF], F32) for t in range(PACK)] for h in range(2)]
 
-        def z_quantize(i):
-            cols = slice(i * P, (i + 1) * P)
-            nc.vector.quantize_mx(out=z_codes[:, cols].bitcast(FP8X4), scales=z_scales[:, cols], in_=z_g[i][:])
+        def fetch_scalar(dst, src):
+            nc.scalar.activation(dst, src, ACT.Copy)
 
-        z_weave(0, nc.vector.tensor_copy)
-        z_weave(1, nc.vector.tensor_copy)
-        z_weave(2, nc.scalar.copy)
-        z_weave(3, nc.scalar.copy)
-        s_bank = [psum.tile([P, N], F32, name="s_bank%d" % i, tag="bank%d" % i) for i in range(PACK)]
+        def b_fetch(h, t, fetch):
+            entries = slice(h * HALF // 16, (h + 1) * HALF // 16)
+            fetch(left[h][t][:], b_win[t][:].indirect(n3_t[:, entries]))
+            fetch(right[h][t][:], b_win[t][:].indirect(n4_t[:, entries]))
+
+        def b_times(h, t):
+            nc.vector.scalar_tensor_tensor(
+                z2_planes[h][:, t, :], left[h][t][:], gb_t[:, t : t + 1], right[h][t][:], ALU.mult, ALU.mult
+            )
+
+        s_bank = [
+            [psum.tile([P, HALF], F32, name="s_bank%d_%d" % (h, i), tag="bank%d" % (PACK * h + i)) for i in range(PACK)]
+            for h in range(2)
+        ]
+
+        def z2_finish(h):
+            cols = slice(h * HALF, (h + 1) * HALF)
+            quantize(z2_codes[:, cols], z2_scales[:, cols], z2_g[h][:])
+            for i in range(PACK):
+                product(s_bank[h][i][:], z_codes, z_scales, i, z2_codes[:, cols], z2_scales[:, cols])
+
+        def s_out(h, i):
+            nc.scalar.activation(s_win[i][:, h * HALF : (h + 1) * HALF], s_bank[h][i][:], ACT.Copy, scale=0.0625)
+
+        for t in range(PACK):
+            b_fetch(0, t, fetch_scalar)
+        b_times(0, 0)
+        quantize(z_codes[:], z_scales[:], z_g[:])
+        for t in range(1, PACK):
+            b_times(0, t)
+        for t in range(PACK - 1):
+            b_fetch(1, t, fetch_scalar)
+        entries = slice(HALF // 16, N // 16)
+        nc.vector.tensor_copy(left[1][3][:], b_win[3][:].indirect(n3_t[:, entries]))
+        weave(z2_g[0][:], z2_planes[0][:])
+        nc.vector.tensor_copy(right[1][3][:], b_win[3][:].indirect(n4_t[:, entries]))
+        z2_finish(0)
+        for t in (3, 0, 1, 2):
+            b_times(1, t)
         for i in range(PACK):
-            z_quantize(i)
-            product(s_bank[i], z_codes, z_scales, i, z2_codes, z2_scales)
+            s_out(0, i)
+        weave(z2_g[1][:], z2_planes[1][:])
+        z2_finish(1)
 
         mb = [sb("mb%d" % i, [P, G], F32) for i in range(PACK)]
         pair = [sb("pair%d" % i, [P, G // 2], F32) for i in range(PACK)]
         top = [sb("top%d" % i, [P, N], F32) for i in range(PACK)]
         res = [sb("res%d" % i, [P, N], F32) for i in range(PACK)]
 
-        def s_out(i):
-            nc.scalar.activation(s_win[i][:, :N], s_bank[i][:], ACT.Copy, scale=0.0625)
-
-        def members(i, lo, hi):
-            return mb[i][:, 4 * lo : 4 * hi], s_win[i][:].indirect(n5_t[:, lo // 4 : hi // 4])
-
-        def fetch_scalar(i):
-            for k in range(2):
-                lo = V_COLS + k * S_COLS
-                dst, src = members(i, lo, lo + S_COLS)
-                nc.scalar.activation(dst, src, ACT.Copy)
-
-        def fetch_vector(i, k):
-            nc.vector.tensor_copy(*members(i, k * V_COLS // 2, (k + 1) * V_COLS // 2))
+        def members(fetch, i, lo, hi):
+            fetch(mb[i][:, 4 * lo : 4 * hi], s_win[i][:].indirect(n5_t[:, lo // 4 : hi // 4]))
 
         def max_pairs(i, lo, hi):
             four = mb[i][:, 4 * lo : 4 * hi].rearrange("p (v a b) -> p v a b", a=2, b=2)
-            two_ = pair[i][:, 2 * lo : 2 * hi].rearrange("p (v b) -> p v b", b=2)
-            nc.vector.tensor_tensor(two_, four[:, :, 0, :], four[:, :, 1, :], ALU.max)
+            both = pair[i][:, 2 * lo : 2 * hi].rearrange("p (v b) -> p v b", b=2)
+            nc.vector.tensor_tensor(both, four[:, :, 0, :], four[:, :, 1, :], ALU.max)
 
         def max_top(i, lo, hi):
-            two_ = pair[i][:, 2 * lo : 2 * hi].rearrange("p (v b) -> p v b", b=2)
-            nc.vector.tensor_tensor(top[i][:, lo:hi], two_[:, :, 0], two_[:, :, 1], ALU.max)
+            both = pair[i][:, 2 * lo : 2 * hi].rearrange("p (v b) -> p v b", b=2)
+            nc.vector.tensor_tensor(top[i][:, lo:hi], both[:, :, 0], both[:, :, 1], ALU.max)
 
         def finish(i, lo, hi):
             nc.vector.tensor_tensor(res[i][:, lo:hi], s_win[i][:, lo:hi], top[i][:, lo:hi], ALU.subtract)
             nc.sync.dma_start(out[i * P : (i + 1) * P, lo:hi], res[i][:, lo:hi])
 
-        s_out(0)
-        for i in range(PACK):
-            if i + 1 < PACK:
-                s_out(i + 1)
-            fetch_scalar(i)
-        for i in range(2):
-            fetch_vector(i, 0)
-            fetch_vector(i, 1)
-        for i in range(2):
-            max_pairs(i, 0, N)
-            fetch_vector(i + 2, 0)
-            max_top(i, 0, N)
-            fetch_vector(i + 2, 1)
-            finish(i, 0, N)
         cuts = [0, V_COLS, V_COLS + S_COLS, N]
-        max_pairs(2, 0, N)
-        max_pairs(3, cuts[0], cuts[1])
-        max_top(2, 0, N)
-        max_top(3, cuts[0], cuts[1])
-        finish(2, 0, N)
-        max_pairs(3, cuts[1], cuts[2])
-        finish(3, cuts[0], cuts[1])
-        max_top(3, cuts[1], cuts[2])
-        max_pairs(3, cuts[2], cuts[3])
-        finish(3, cuts[1], cuts[2])
-        max_top(3, cuts[2], cuts[3])
-        finish(3, cuts[2], cuts[3])
+        last = PACK - 1
+        for i in range(last):
+            s_out(1, i)
+        for i in range(PACK):
+            members(fetch_scalar, i, cuts[1], cuts[2])
+            members(fetch_scalar, i, cuts[2], cuts[3])
+            if i == 0:
+                s_out(1, last)
+        for i in range(last):
+            members(nc.vector.tensor_copy, i, cuts[0], cuts[1])
+        max_pairs(0, 0, N)
+        members(nc.vector.tensor_copy, last, 0, V_COLS // 2)
+        max_top(0, 0, N)
+        members(nc.vector.tensor_copy, last, V_COLS // 2, V_COLS)
+        finish(0, 0, N)
+        for step in (max_pairs, max_top, finish):
+            step(1, 0, N)
+            step(last, cuts[0], cuts[1])
+        for step in (max_pairs, max_top, finish):
+            step(2, 0, N)
+            step(last, cuts[1], cuts[2])
+        for step in (max_pairs, max_top, finish):
+            step(last, cuts[2], cuts[3])

@@ -21,6 +21,7 @@ W = 384
 G = 2048
 A_WIN = 768
 S_WIN = 768
+CAST_SPLIT = 84
 V_COLS = 144
 S_COLS = (N - V_COLS) // 2
 
@@ -89,8 +90,8 @@ def tile_picked_hkqktanhprodgmaxd_none_p_kernel(
         nc.vector.tensor_copy(xb_words[:], xw[:].bitcast(U32).indirect(two_t[:]))
 
         def cast_views(raw, grouped, lo, hi):
-            src = raw[:].rearrange("p j (m t) -> p m j t", t=PACK)[:, lo:hi]
-            dst = grouped[:].rearrange("p (t m j) -> p m j t", t=PACK, j=PACK)[:, lo:hi]
+            src = raw[:].rearrange("p j (m t) -> p m t j", t=PACK)[:, lo:hi]
+            dst = grouped[:].rearrange("p (t m j) -> p m t j", t=PACK, j=PACK)[:, lo:hi]
             return dst, src
 
         def quantize(codes, scales, grouped):
@@ -111,7 +112,8 @@ def tile_picked_hkqktanhprodgmaxd_none_p_kernel(
         w1_g = sb("w1_g", [P, PACK * N], BF16)
         w1_codes = sb("w1_codes", [P, N], U32)
         w1_scales = sb("w1_scales", [P, N], U8)
-        nc.vector.tensor_copy(*cast_views(w1_raw, w1_g, 0, P))
+        nc.vector.tensor_copy(*cast_views(w1_raw, w1_g, 0, CAST_SPLIT))
+        nc.scalar.copy(*cast_views(w1_raw, w1_g, CAST_SPLIT, P))
         a_bank = [psum.tile([P, N], F32, name="a_bank%d" % t, tag="bank%d" % t) for t in range(PACK)]
         for t in range(PACK):
             cols = slice(t * P, (t + 1) * P)

@@ -123,30 +123,45 @@ def tile_picked_hkqktanhprodgmaxd_none_p_kernel(
         w2_g = sb("w2_g", [P, PACK * N], BF16)
         w2_codes = sb("w2_codes", [P, N], U32)
         w2_scales = sb("w2_scales", [P, N], U8)
-        ga2 = sb("ga2", [P, PACK], F32)
         b_bank = [psum.tile([P, N], F32, name="b_bank%d" % t, tag="bank%d" % (PACK + t)) for t in range(PACK)]
         sig = [sb("sig%d" % t, [P, W], F32) for t in range(PACK)]
-        old = [sb("old%d" % t, [P, W], F32) for t in range(PACK)]
+        upd = [sb("upd%d" % t, [P, W], F32) for t in range(PACK)]
         z_planes = sb("z_planes", [P, PACK, N], BF16)
 
         def a_out(t):
             nc.vector.tensor_scalar(a_win[t][:, :N], a_bank[t][:], 0.5, None, ALU.mult)
 
+        def a_sigmoid(t):
+            nc.scalar.activation(sig[t][:], a_win[t][:].indirect(n2_t[:]), ACT.Sigmoid, scale=-4.0)
+
+        def a_add(t):
+            nc.vector.tensor_tensor(upd[t][:], a_win[t][:].indirect(n1_t[:]), sig[t][:], ALU.add)
+
+        def a_put(t):
+            nc.scalar.activation(a_win[t][:].indirect(n1_t[:]), upd[t][:], ACT.Copy, bias=-0.5)
+
+        def z_scale(t):
+            nc.vector.tensor_scalar(z_planes[:, t, :], a_win[t][:, :N], ga_t[:, t : t + 1], 2.0, ALU.mult, ALU.mult)
+
         a_out(0)
         a_out(1)
-        nc.vector.tensor_copy(*cast_views(w2_raw, w2_g, 0, P))
+        a_sigmoid(0)
+        a_sigmoid(1)
+        a_add(0)
+        a_put(0)
         a_out(2)
+        nc.vector.tensor_copy(*cast_views(w2_raw, w2_g, 0, P))
+        a_out(3)
+        a_sigmoid(2)
+        a_sigmoid(3)
+        a_add(1)
         quantize(w2_codes[:], w2_scales[:], w2_g[:])
         for t in range(PACK):
             product(b_bank[t][:], w2_codes, w2_scales, t, xb_words[:], xb_scales[:])
-        a_out(3)
-        nc.vector.tensor_scalar(ga2[:], ga_t[:], 2.0, None, ALU.mult)
-        for t in range(PACK):
-            nc.scalar.activation(sig[t][:], a_win[t][:].indirect(n2_t[:]), ACT.Sigmoid, scale=-4.0)
-            nc.scalar.activation(old[t][:], a_win[t][:].indirect(n1_t[:]), ACT.Copy, bias=-0.5)
-            nc.vector.tensor_tensor(a_win[t][:].indirect(n1_t[:]), old[t][:], sig[t][:], ALU.add)
-        for t in range(PACK):
-            nc.vector.tensor_scalar(z_planes[:, t, :], a_win[t][:, :N], ga2[:, t : t + 1], None, ALU.mult)
+        a_add(2)
+        a_add(3)
+        for t in range(1, PACK):
+            a_put(t)
 
         def weave(grouped, planes):
             nc.vector.tensor_copy(
@@ -156,11 +171,7 @@ def tile_picked_hkqktanhprodgmaxd_none_p_kernel(
         z_g = sb("z_g", [P, PACK * N], BF16)
         z_codes = sb("z_codes", [P, N], U32)
         z_scales = sb("z_scales", [P, N], U8)
-        weave(z_g[:], z_planes[:])
-
         b_win = [sb("b_win%d" % t, [P, N], F32) for t in range(PACK)]
-        for t in range(PACK):
-            nc.scalar.copy(b_win[t][:], b_bank[t][:])
         z2_codes = sb("z2_codes", [P, N], U32)
         z2_scales = sb("z2_scales", [P, N], U8)
         z2_planes = [sb("z2_planes%d" % h, [P, PACK, HALF], BF16) for h in range(2)]
@@ -171,10 +182,29 @@ def tile_picked_hkqktanhprodgmaxd_none_p_kernel(
         def fetch_scalar(dst, src):
             nc.scalar.activation(dst, src, ACT.Copy)
 
-        def b_fetch(h, t, fetch):
-            entries = slice(h * HALF // 16, (h + 1) * HALF // 16)
-            fetch(left[h][t][:], b_win[t][:].indirect(n3_t[:, entries]))
-            fetch(right[h][t][:], b_win[t][:].indirect(n4_t[:, entries]))
+        def b_at(t, picks, h):
+            return b_win[t][:].indirect(picks[:, h * HALF // 16 : (h + 1) * HALF // 16])
+
+        on_vector = (0, 1)
+        on_scalar = (2, 3)
+        for t in on_vector:
+            nc.vector.tensor_copy(b_win[t][:], b_bank[t][:])
+        for t in on_scalar:
+            nc.scalar.copy(b_win[t][:], b_bank[t][:])
+        for h in range(2):
+            for t in on_scalar:
+                fetch_scalar(left[h][t][:], b_at(t, n3_t, h))
+                fetch_scalar(right[h][t][:], b_at(t, n4_t, h))
+        for h in range(2):
+            for t in on_vector:
+                nc.vector.tensor_copy(left[h][t][:], b_at(t, n3_t, h))
+            for t in on_vector:
+                nc.vector.tensor_tensor(right[h][t][:], b_at(t, n4_t, h), left[h][t][:], ALU.mult)
+        for h in range(2):
+            for t in on_vector:
+                nc.vector.tensor_scalar(z2_planes[h][:, t, :], right[h][t][:], gb_t[:, t : t + 1], None, ALU.mult)
+        for t in range(PACK):
+            z_scale(t)
 
         def b_times(h, t):
             nc.vector.scalar_tensor_tensor(
@@ -195,21 +225,14 @@ def tile_picked_hkqktanhprodgmaxd_none_p_kernel(
         def s_out(h, i):
             nc.scalar.activation(s_win[i][:, h * HALF : (h + 1) * HALF], s_bank[h][i][:], ACT.Copy, scale=0.0625)
 
-        for t in range(PACK):
-            b_fetch(0, t, fetch_scalar)
-        b_times(0, 0)
+        b_times(0, 2)
+        weave(z_g[:], z_planes[:])
+        b_times(0, 3)
         quantize(z_codes[:], z_scales[:], z_g[:])
-        for t in range(1, PACK):
-            b_times(0, t)
-        for t in range(PACK - 1):
-            b_fetch(1, t, fetch_scalar)
-        entries = slice(HALF // 16, N // 16)
-        nc.vector.tensor_copy(left[1][3][:], b_win[3][:].indirect(n3_t[:, entries]))
         weave(z2_g[0][:], z2_planes[0][:])
-        nc.vector.tensor_copy(right[1][3][:], b_win[3][:].indirect(n4_t[:, entries]))
+        b_times(1, 2)
         z2_finish(0)
-        for t in (3, 0, 1, 2):
-            b_times(1, t)
+        b_times(1, 3)
         for i in range(PACK):
             s_out(0, i)
         weave(z2_g[1][:], z2_planes[1][:])
@@ -240,11 +263,14 @@ def tile_picked_hkqktanhprodgmaxd_none_p_kernel(
         last = PACK - 1
         for i in range(last):
             s_out(1, i)
-        for i in range(PACK):
+        for i in range(last):
             members(fetch_scalar, i, cuts[1], cuts[2])
             members(fetch_scalar, i, cuts[2], cuts[3])
             if i == 0:
                 s_out(1, last)
+        ends = [V_COLS, 320, 448, N]
+        for k in range(3):
+            members(fetch_scalar, last, ends[k], ends[k + 1])
         for i in range(last):
             members(nc.vector.tensor_copy, i, cuts[0], cuts[1])
         max_pairs(0, 0, N)
@@ -257,6 +283,14 @@ def tile_picked_hkqktanhprodgmaxd_none_p_kernel(
             step(last, cuts[0], cuts[1])
         for step in (max_pairs, max_top, finish):
             step(2, 0, N)
-            step(last, cuts[1], cuts[2])
-        for step in (max_pairs, max_top, finish):
-            step(last, cuts[2], cuts[3])
+            step(last, ends[0], ends[1])
+        max_pairs(last, ends[1], ends[2])
+        max_top(last, ends[1], ends[2])
+        nc.vector.tensor_reduce(
+            top[last][:, ends[2] :],
+            mb[last][:, 4 * ends[2] :].rearrange("p (v a) -> p v a", a=4),
+            mybir.AxisListType.X,
+            ALU.max,
+        )
+        finish(last, ends[1], ends[2])
+        finish(last, ends[2], ends[3])

@@ -14,18 +14,23 @@ ACT = mybir.ActivationFunctionType
 
 P = 128
 PACK = 4
-T = 2048
+TOKENS = 2048
 N = 512
-HALF = 256
-W = 384
-G = 2048
-A_WIN = 768
-S_WIN = 768
-CAST_SPLIT = 84
-V_COLS = 144
-S_COLS = (N - V_COLS) // 2
+UPDATED = 384
+MEMBERS = 4
+BLOCKS = 16
+WINDOW = 768
 
-FLOPS = 3 * 2 * 512 * 512 * 512
+CAST_SPLIT = 84
+VECTOR_PLANES = (0, 1)
+SCALAR_PLANES = (2, 3)
+VECTOR_COLS = 160
+
+Z2_PARTS = ((0, 256), (256, 384), (384, 512))
+EVEN_CUTS = (VECTOR_COLS, (VECTOR_COLS + N) // 2, N)
+LAST_CUTS = (VECTOR_COLS, 320, 448, N)
+
+FLOPS = 3 * 2 * N * N * N
 
 
 def tile_picked_hkqktanhprodgmaxd_none_p_kernel(
@@ -45,26 +50,26 @@ def tile_picked_hkqktanhprodgmaxd_none_p_kernel(
             nc.sync.dma_start(tile[:], src)
             return tile
 
-        a_win = [sb("a_win%d" % t, [P, A_WIN], F32) for t in range(PACK)]
-        s_win = [sb("s_win%d" % t, [P, S_WIN], F32) for t in range(PACK)]
+        a_win = [sb("a_win%d" % t, [P, WINDOW], F32) for t in range(PACK)]
+        s_win = [sb("s_win%d" % i, [P, WINDOW], F32) for i in range(PACK)]
         for win in a_win + s_win:
             nc.vector.memset(win[:, N:], 0.0)
 
-        xs = sb("xs", [P, T], U8)
-        rows = x_scales[0].bitcast(I32).rearrange("(g e) c -> e g c", e=2)
-        for r in range(2):
-            nc.sync.dma_start(xs[:].bitcast(I32)[r:P:2, :], rows[r].unsqueeze(1).to_broadcast([8, 8, T // 4]))
+        xs = sb("xs", [P, TOKENS], U8)
+        nc.sync.dma_start(
+            xs[:].bitcast(I32), x_scales[0].bitcast(I32).unsqueeze(1).to_broadcast([BLOCKS, P // BLOCKS, TOKENS // 4])
+        )
         offs_t = load_list("offs_t", offs)
         two_t = load_list("two_t", two)
         n2_t = load_list("n2_t", n2)
         n1_t = load_list("n1_t", n1)
-        xw = sb("xw", [P, T], I32)
+        n3_t = load_list("n3_t", n3)
+        xw = sb("xw", [P, TOKENS], I32)
         nc.sync.dma_start(xw[:], x_words[0].rearrange("p n t -> p (n t)").bitcast(I32))
         w1_raw = sb("w1_raw", [P, PACK, N], F32)
         nc.sync.dma_start(w1_raw[:], w1.rearrange("(p j) c -> p j c", j=PACK))
         w2_raw = sb("w2_raw", [P, PACK, N], F32)
         nc.sync.dma_start(w2_raw[:], w2.rearrange("(p j) c -> p j c", j=PACK))
-        n3_t = load_list("n3_t", n3)
         n4_t = load_list("n4_t", n4)
         n5_t = load_list("n5_t", n5)
         ga_t = sb("ga_t", [P, PACK], F32)
@@ -77,28 +82,29 @@ def tile_picked_hkqktanhprodgmaxd_none_p_kernel(
 
         def pick_scales(name, picks, queue):
             picked = sb(name + "_bytes", [P, N], U8)
-            plane = sb(name + "_scales", [P, N], U8)
+            scales = sb(name + "_scales", [P, N], U8)
             nc.vector.tensor_copy(picked[:], xs[:].indirect(picks[:]))
-            nc.vector.tensor_copy(plane[:].bitcast(I32), picked[:].bitcast(I32))
-            for r in range(2):
-                queue.dma_start(plane[:].bitcast(I32)[2 + r : P : 32, :], picked[:].bitcast(I32)[16 + r : P : 32, :])
-            return plane
+            nc.vector.tensor_copy(scales[:].bitcast(I32), picked[:].bitcast(I32))
+            for r in range(1, 4):
+                queue.dma_start(scales[:].bitcast(I32)[r:P:32, :], picked[:].bitcast(I32)[8 * r : P : 32, :])
+            return scales
 
         xa_scales = pick_scales("xa", offs_t, nc.scalar)
         xb_scales = pick_scales("xb", two_t, nc.sync)
         nc.vector.tensor_copy(xa_words[:], xw[:].bitcast(U32).indirect(offs_t[:]))
         nc.vector.tensor_copy(xb_words[:], xw[:].bitcast(U32).indirect(two_t[:]))
 
-        def cast_views(raw, grouped, lo, hi):
-            src = raw[:].rearrange("p j (m t) -> p m t j", t=PACK)[:, lo:hi]
-            dst = grouped[:].rearrange("p (t m j) -> p m t j", t=PACK, j=PACK)[:, lo:hi]
-            return dst, src
+        def deal_weights(copy, raw, grouped, lo, hi):
+            copy(
+                grouped[:].rearrange("p (t m j) -> p m t j", t=PACK, j=PACK)[:, lo:hi],
+                raw[:].rearrange("p j (m t) -> p m t j", t=PACK)[:, lo:hi],
+            )
 
         def quantize(codes, scales, grouped):
             nc.vector.quantize_mx(out=codes.bitcast(FP8X4), scales=scales, in_=grouped)
 
-        def product(acc, l_codes, l_scales, blk, r_codes, r_scales):
-            cols = slice(blk * P, (blk + 1) * P)
+        def product(acc, l_codes, l_scales, block, r_codes, r_scales):
+            cols = slice(block * P, (block + 1) * P)
             nc.tensor.matmul_mx(
                 out=acc,
                 lhsT=l_codes[:, cols].bitcast(FP8X4),
@@ -112,8 +118,8 @@ def tile_picked_hkqktanhprodgmaxd_none_p_kernel(
         w1_g = sb("w1_g", [P, PACK * N], BF16)
         w1_codes = sb("w1_codes", [P, N], U32)
         w1_scales = sb("w1_scales", [P, N], U8)
-        nc.vector.tensor_copy(*cast_views(w1_raw, w1_g, 0, CAST_SPLIT))
-        nc.scalar.copy(*cast_views(w1_raw, w1_g, CAST_SPLIT, P))
+        deal_weights(nc.vector.tensor_copy, w1_raw, w1_g, 0, CAST_SPLIT)
+        deal_weights(nc.scalar.copy, w1_raw, w1_g, CAST_SPLIT, P)
         a_bank = [psum.tile([P, N], F32, name="a_bank%d" % t, tag="bank%d" % t) for t in range(PACK)]
         for t in range(PACK):
             cols = slice(t * P, (t + 1) * P)
@@ -124,8 +130,8 @@ def tile_picked_hkqktanhprodgmaxd_none_p_kernel(
         w2_codes = sb("w2_codes", [P, N], U32)
         w2_scales = sb("w2_scales", [P, N], U8)
         b_bank = [psum.tile([P, N], F32, name="b_bank%d" % t, tag="bank%d" % (PACK + t)) for t in range(PACK)]
-        sig = [sb("sig%d" % t, [P, W], F32) for t in range(PACK)]
-        upd = [sb("upd%d" % t, [P, W], F32) for t in range(PACK)]
+        sig = [sb("sig%d" % t, [P, UPDATED], F32) for t in range(PACK)]
+        upd = [sb("upd%d" % t, [P, UPDATED], F32) for t in range(PACK)]
         z_planes = sb("z_planes", [P, PACK, N], BF16)
 
         def a_out(t):
@@ -140,9 +146,6 @@ def tile_picked_hkqktanhprodgmaxd_none_p_kernel(
         def a_put(t):
             nc.scalar.activation(a_win[t][:].indirect(n1_t[:]), upd[t][:], ACT.Copy, bias=-0.5)
 
-        def z_scale(t):
-            nc.vector.tensor_scalar(z_planes[:, t, :], a_win[t][:, :N], ga_t[:, t : t + 1], 2.0, ALU.mult, ALU.mult)
-
         a_out(0)
         a_out(1)
         a_sigmoid(0)
@@ -150,7 +153,7 @@ def tile_picked_hkqktanhprodgmaxd_none_p_kernel(
         a_add(0)
         a_put(0)
         a_out(2)
-        nc.vector.tensor_copy(*cast_views(w2_raw, w2_g, 0, P))
+        deal_weights(nc.vector.tensor_copy, w2_raw, w2_g, 0, P)
         a_out(3)
         a_sigmoid(2)
         a_sigmoid(3)
@@ -163,91 +166,103 @@ def tile_picked_hkqktanhprodgmaxd_none_p_kernel(
         for t in range(1, PACK):
             a_put(t)
 
-        def weave(grouped, planes):
-            nc.vector.tensor_copy(
-                grouped.rearrange("p (c i t) -> p c t i", i=4, t=PACK), planes.rearrange("p t (c i) -> p c t i", i=4)
-            )
-
         z_g = sb("z_g", [P, PACK * N], BF16)
         z_codes = sb("z_codes", [P, N], U32)
         z_scales = sb("z_scales", [P, N], U8)
         b_win = [sb("b_win%d" % t, [P, N], F32) for t in range(PACK)]
         z2_codes = sb("z2_codes", [P, N], U32)
         z2_scales = sb("z2_scales", [P, N], U8)
-        z2_planes = [sb("z2_planes%d" % h, [P, PACK, HALF], BF16) for h in range(2)]
-        z2_g = [sb("z2_g%d" % h, [P, PACK * HALF], BF16) for h in range(2)]
-        left = [[sb("left%d_%d" % (h, t), [P, HALF], F32) for t in range(PACK)] for h in range(2)]
-        right = [[sb("right%d_%d" % (h, t), [P, HALF], F32) for t in range(PACK)] for h in range(2)]
+        z2_planes = [sb("z2_planes%d" % k, [P, PACK, hi - lo], BF16) for k, (lo, hi) in enumerate(Z2_PARTS)]
+        z2_g = [sb("z2_g%d" % k, [P, PACK * (hi - lo)], BF16) for k, (lo, hi) in enumerate(Z2_PARTS)]
+        at_n3 = [sb("at_n3_%d" % t, [P, N], F32) for t in range(PACK)]
+        at_n4 = [sb("at_n4_%d" % t, [P, N], F32) for t in range(PACK)]
 
         def fetch_scalar(dst, src):
             nc.scalar.activation(dst, src, ACT.Copy)
 
-        def b_at(t, picks, h):
-            return b_win[t][:].indirect(picks[:, h * HALF // 16 : (h + 1) * HALF // 16])
+        def b_at(t, picks, lo, hi):
+            return b_win[t][:].indirect(picks[:, lo // 16 : hi // 16])
 
-        on_vector = (0, 1)
-        on_scalar = (2, 3)
-        for t in on_vector:
+        for t in VECTOR_PLANES:
             nc.vector.tensor_copy(b_win[t][:], b_bank[t][:])
-        for t in on_scalar:
+        for t in SCALAR_PLANES:
             nc.scalar.copy(b_win[t][:], b_bank[t][:])
-        for h in range(2):
-            for t in on_scalar:
-                fetch_scalar(left[h][t][:], b_at(t, n3_t, h))
-                fetch_scalar(right[h][t][:], b_at(t, n4_t, h))
-        for h in range(2):
-            for t in on_vector:
-                nc.vector.tensor_copy(left[h][t][:], b_at(t, n3_t, h))
-            for t in on_vector:
-                nc.vector.tensor_tensor(right[h][t][:], b_at(t, n4_t, h), left[h][t][:], ALU.mult)
-        for h in range(2):
-            for t in on_vector:
-                nc.vector.tensor_scalar(z2_planes[h][:, t, :], right[h][t][:], gb_t[:, t : t + 1], None, ALU.mult)
-        for t in range(PACK):
-            z_scale(t)
+        for lo, hi in Z2_PARTS:
+            for t in SCALAR_PLANES:
+                fetch_scalar(at_n3[t][:, lo:hi], b_at(t, n3_t, lo, hi))
+                fetch_scalar(at_n4[t][:, lo:hi], b_at(t, n4_t, lo, hi))
+        for lo, hi in ((0, N // 2), (N // 2, N)):
+            for t in VECTOR_PLANES:
+                nc.vector.tensor_copy(at_n3[t][:, lo:hi], b_at(t, n3_t, lo, hi))
+            for t in VECTOR_PLANES:
+                nc.vector.tensor_tensor(at_n4[t][:, lo:hi], b_at(t, n4_t, lo, hi), at_n3[t][:, lo:hi], ALU.mult)
 
-        def b_times(h, t):
+        for k, (lo, hi) in enumerate(Z2_PARTS):
+            for t in VECTOR_PLANES:
+                nc.vector.tensor_scalar(z2_planes[k][:, t, :], at_n4[t][:, lo:hi], gb_t[:, t : t + 1], None, ALU.mult)
+        for t in range(PACK):
+            nc.vector.tensor_scalar(z_planes[:, t, :], a_win[t][:, :N], ga_t[:, t : t + 1], 2.0, ALU.mult, ALU.mult)
+
+        def z2_times(k, t):
+            lo, hi = Z2_PARTS[k]
             nc.vector.scalar_tensor_tensor(
-                z2_planes[h][:, t, :], left[h][t][:], gb_t[:, t : t + 1], right[h][t][:], ALU.mult, ALU.mult
+                z2_planes[k][:, t, :], at_n3[t][:, lo:hi], gb_t[:, t : t + 1], at_n4[t][:, lo:hi], ALU.mult, ALU.mult
+            )
+
+        def weave(grouped, planes):
+            nc.vector.tensor_copy(
+                grouped[:].rearrange("p (c i t) -> p c t i", i=4, t=PACK),
+                planes[:].rearrange("p t (c i) -> p c t i", i=4),
             )
 
         s_bank = [
-            [psum.tile([P, HALF], F32, name="s_bank%d_%d" % (h, i), tag="bank%d" % (PACK * h + i)) for i in range(PACK)]
-            for h in range(2)
+            [
+                psum.tile([P, hi - lo], F32, name="s_bank%d_%d" % (k, i), tag="bank%d" % (PACK * (k % 2) + i))
+                for i in range(PACK)
+            ]
+            for k, (lo, hi) in enumerate(Z2_PARTS)
         ]
 
-        def z2_finish(h):
-            cols = slice(h * HALF, (h + 1) * HALF)
-            quantize(z2_codes[:, cols], z2_scales[:, cols], z2_g[h][:])
+        def s_products(k):
+            cols = slice(*Z2_PARTS[k])
+            quantize(z2_codes[:, cols], z2_scales[:, cols], z2_g[k][:])
             for i in range(PACK):
-                product(s_bank[h][i][:], z_codes, z_scales, i, z2_codes[:, cols], z2_scales[:, cols])
+                product(s_bank[k][i][:], z_codes, z_scales, i, z2_codes[:, cols], z2_scales[:, cols])
 
-        def s_out(h, i):
-            nc.scalar.activation(s_win[i][:, h * HALF : (h + 1) * HALF], s_bank[h][i][:], ACT.Copy, scale=0.0625)
+        def s_out(k, i):
+            nc.scalar.activation(s_win[i][:, slice(*Z2_PARTS[k])], s_bank[k][i][:], ACT.Copy, scale=0.0625)
 
-        b_times(0, 2)
-        weave(z_g[:], z_planes[:])
-        b_times(0, 3)
+        first, second = SCALAR_PLANES
+        z2_times(0, first)
+        weave(z_g, z_planes)
+        z2_times(0, second)
         quantize(z_codes[:], z_scales[:], z_g[:])
-        weave(z2_g[0][:], z2_planes[0][:])
-        b_times(1, 2)
-        z2_finish(0)
-        b_times(1, 3)
+        weave(z2_g[0], z2_planes[0])
+        z2_times(1, first)
+        s_products(0)
+        z2_times(1, second)
+        z2_times(2, first)
         for i in range(PACK):
             s_out(0, i)
-        weave(z2_g[1][:], z2_planes[1][:])
-        z2_finish(1)
+        weave(z2_g[1], z2_planes[1])
+        z2_times(2, second)
+        s_products(1)
+        for i in range(PACK):
+            s_out(1, i)
+        weave(z2_g[2], z2_planes[2])
+        s_products(2)
 
-        mb = [sb("mb%d" % i, [P, G], F32) for i in range(PACK)]
-        pair = [sb("pair%d" % i, [P, G // 2], F32) for i in range(PACK)]
+        mb = [sb("mb%d" % i, [P, MEMBERS * N], F32) for i in range(PACK)]
+        pair = [sb("pair%d" % i, [P, 2 * N], F32) for i in range(PACK)]
         top = [sb("top%d" % i, [P, N], F32) for i in range(PACK)]
         res = [sb("res%d" % i, [P, N], F32) for i in range(PACK)]
 
         def members(fetch, i, lo, hi):
-            fetch(mb[i][:, 4 * lo : 4 * hi], s_win[i][:].indirect(n5_t[:, lo // 4 : hi // 4]))
+            entries = slice(MEMBERS * lo // 16, MEMBERS * hi // 16)
+            fetch(mb[i][:, MEMBERS * lo : MEMBERS * hi], s_win[i][:].indirect(n5_t[:, entries]))
 
         def max_pairs(i, lo, hi):
-            four = mb[i][:, 4 * lo : 4 * hi].rearrange("p (v a b) -> p v a b", a=2, b=2)
+            four = mb[i][:, MEMBERS * lo : MEMBERS * hi].rearrange("p (v a b) -> p v a b", a=2, b=2)
             both = pair[i][:, 2 * lo : 2 * hi].rearrange("p (v b) -> p v b", b=2)
             nc.vector.tensor_tensor(both, four[:, :, 0, :], four[:, :, 1, :], ALU.max)
 
@@ -259,38 +274,37 @@ def tile_picked_hkqktanhprodgmaxd_none_p_kernel(
             nc.vector.tensor_tensor(res[i][:, lo:hi], s_win[i][:, lo:hi], top[i][:, lo:hi], ALU.subtract)
             nc.sync.dma_start(out[i * P : (i + 1) * P, lo:hi], res[i][:, lo:hi])
 
-        cuts = [0, V_COLS, V_COLS + S_COLS, N]
         last = PACK - 1
         for i in range(last):
-            s_out(1, i)
+            s_out(2, i)
         for i in range(last):
-            members(fetch_scalar, i, cuts[1], cuts[2])
-            members(fetch_scalar, i, cuts[2], cuts[3])
+            members(fetch_scalar, i, EVEN_CUTS[0], EVEN_CUTS[1])
+            members(fetch_scalar, i, EVEN_CUTS[1], EVEN_CUTS[2])
             if i == 0:
-                s_out(1, last)
-        ends = [V_COLS, 320, 448, N]
+                s_out(2, last)
         for k in range(3):
-            members(fetch_scalar, last, ends[k], ends[k + 1])
+            members(fetch_scalar, last, LAST_CUTS[k], LAST_CUTS[k + 1])
+
         for i in range(last):
-            members(nc.vector.tensor_copy, i, cuts[0], cuts[1])
+            members(nc.vector.tensor_copy, i, 0, VECTOR_COLS)
         max_pairs(0, 0, N)
-        members(nc.vector.tensor_copy, last, 0, V_COLS // 2)
+        members(nc.vector.tensor_copy, last, 0, VECTOR_COLS // 2)
         max_top(0, 0, N)
-        members(nc.vector.tensor_copy, last, V_COLS // 2, V_COLS)
+        members(nc.vector.tensor_copy, last, VECTOR_COLS // 2, VECTOR_COLS)
         finish(0, 0, N)
         for step in (max_pairs, max_top, finish):
             step(1, 0, N)
-            step(last, cuts[0], cuts[1])
+            step(last, 0, LAST_CUTS[0])
         for step in (max_pairs, max_top, finish):
             step(2, 0, N)
-            step(last, ends[0], ends[1])
-        max_pairs(last, ends[1], ends[2])
-        max_top(last, ends[1], ends[2])
+            step(last, LAST_CUTS[0], LAST_CUTS[1])
+        max_pairs(last, LAST_CUTS[1], LAST_CUTS[2])
+        max_top(last, LAST_CUTS[1], LAST_CUTS[2])
         nc.vector.tensor_reduce(
-            top[last][:, ends[2] :],
-            mb[last][:, 4 * ends[2] :].rearrange("p (v a) -> p v a", a=4),
+            top[last][:, LAST_CUTS[2] :],
+            mb[last][:, MEMBERS * LAST_CUTS[2] :].rearrange("p (v a) -> p v a", a=MEMBERS),
             mybir.AxisListType.X,
             ALU.max,
         )
-        finish(last, ends[1], ends[2])
-        finish(last, ends[2], ends[3])
+        finish(last, LAST_CUTS[1], LAST_CUTS[2])
+        finish(last, LAST_CUTS[2], LAST_CUTS[3])

from contextlib import ExitStack

import concourse.mybir as mybir

F32 = mybir.dt.float32
BF16 = mybir.dt.bfloat16
I32 = mybir.dt.int32
U32 = mybir.dt.uint32
U16 = mybir.dt.uint16
U8 = mybir.dt.uint8
FP8X4 = mybir.dt.float8_e4m3fn_x4
ALU = mybir.AluOpType
ACT = mybir.ActivationFunctionType

P = 128
PACK = 4
TOKENS = 2048
N = 512
UPDATED = 384
MEMBERS = 4
BLOCKS = 16
WINDOW = 768

CAST_SPLIT = 84
VECTOR_PLANES = (0, 1)
SCALAR_PLANES = (2, 3)
VECTOR_COLS = 160

Z2_PARTS = ((0, 256), (256, 384), (384, 512))
EVEN_CUTS = (VECTOR_COLS, (VECTOR_COLS + N) // 2, N)
LAST_CUTS = (VECTOR_COLS, 320, 448, N)

FLOPS = 3 * 2 * N * N * N


def tile_picked_hkqktanhprodgmaxd_none_p_kernel(
    tc, x_words, x_scales, w1, w2, ga, gb, offs, two, n1, n2, n3, n4, n5, out
):
    nc = tc.nc
    with ExitStack() as ctx:
        lists = ctx.enter_context(tc.tile_pool(name="lists", bufs=1))
        keep = ctx.enter_context(tc.tile_pool(name="keep", bufs=1))
        psum = ctx.enter_context(tc.psum_pool(name="psum", bufs=1))

        def sb(name, shape, dtype):
            return keep.tile(shape, dtype, name=name, align_bytes=64)

        def load_list(name, src):
            tile = lists.tile(list(src.shape), U16, name=name)
            nc.sync.dma_start(tile[:], src)
            return tile

        a_win = [sb("a_win%d" % t, [P, WINDOW], F32) for t in range(PACK)]
        s_win = [sb("s_win%d" % i, [P, WINDOW], F32) for i in range(PACK)]
        for win in a_win + s_win:
            nc.vector.memset(win[:, N:], 0.0)

        xs = sb("xs", [P, TOKENS], U8)
        nc.sync.dma_start(
            xs[:].bitcast(I32), x_scales[0].bitcast(I32).unsqueeze(1).to_broadcast([BLOCKS, P // BLOCKS, TOKENS // 4])
        )
        offs_t = load_list("offs_t", offs)
        two_t = load_list("two_t", two)
        n2_t = load_list("n2_t", n2)
        n1_t = load_list("n1_t", n1)
        n3_t = load_list("n3_t", n3)
        xw = sb("xw", [P, TOKENS], I32)
        nc.sync.dma_start(xw[:], x_words[0].rearrange("p n t -> p (n t)").bitcast(I32))
        w1_raw = sb("w1_raw", [P, PACK, N], F32)
        nc.sync.dma_start(w1_raw[:], w1.rearrange("(p j) c -> p j c", j=PACK))
        w2_raw = sb("w2_raw", [P, PACK, N], F32)
        nc.sync.dma_start(w2_raw[:], w2.rearrange("(p j) c -> p j c", j=PACK))
        n4_t = load_list("n4_t", n4)
        n5_t = load_list("n5_t", n5)
        ga_t = sb("ga_t", [P, PACK], F32)
        gb_t = sb("gb_t", [P, PACK], F32)
        nc.gpsimd.dma_start(ga_t[:], ga.rearrange("(p t) o -> p (t o)", t=PACK))
        nc.gpsimd.dma_start(gb_t[:], gb.rearrange("(p t) o -> p (t o)", t=PACK))

        xa_words = sb("xa_words", [P, N], U32)
        xb_words = sb("xb_words", [P, N], U32)

        def pick_scales(name, picks, queue):
            picked = sb(name + "_bytes", [P, N], U8)
            scales = sb(name + "_scales", [P, N], U8)
            nc.vector.tensor_copy(picked[:], xs[:].indirect(picks[:]))
            nc.vector.tensor_copy(scales[:].bitcast(I32), picked[:].bitcast(I32))
            for r in range(1, 4):
                queue.dma_start(scales[:].bitcast(I32)[r:P:32, :], picked[:].bitcast(I32)[8 * r : P : 32, :])
            return scales

        xa_scales = pick_scales("xa", offs_t, nc.scalar)
        xb_scales = pick_scales("xb", two_t, nc.sync)
        nc.vector.tensor_copy(xa_words[:], xw[:].bitcast(U32).indirect(offs_t[:]))
        nc.vector.tensor_copy(xb_words[:], xw[:].bitcast(U32).indirect(two_t[:]))

        def deal_weights(copy, raw, grouped, lo, hi):
            copy(
                grouped[:].rearrange("p (t m j) -> p m t j", t=PACK, j=PACK)[:, lo:hi],
                raw[:].rearrange("p j (m t) -> p m t j", t=PACK)[:, lo:hi],
            )

        def quantize(codes, scales, grouped):
            nc.vector.quantize_mx(out=codes.bitcast(FP8X4), scales=scales, in_=grouped)

        def product(acc, l_codes, l_scales, block, r_codes, r_scales):
            cols = slice(block * P, (block + 1) * P)
            nc.tensor.matmul_mx(
                out=acc,
                lhsT=l_codes[:, cols].bitcast(FP8X4),
                lhsT_scale=l_scales[:, cols],
                rhs=r_codes.bitcast(FP8X4),
                rhs_scale=r_scales,
                start=True,
                stop=True,
            )

        w1_g = sb("w1_g", [P, PACK * N], BF16)
        w1_codes = sb("w1_codes", [P, N], U32)
        w1_scales = sb("w1_scales", [P, N], U8)
        deal_weights(nc.vector.tensor_copy, w1_raw, w1_g, 0, CAST_SPLIT)
        deal_weights(nc.scalar.copy, w1_raw, w1_g, CAST_SPLIT, P)
        a_bank = [psum.tile([P, N], F32, name="a_bank%d" % t, tag="bank%d" % t) for t in range(PACK)]
        for t in range(PACK):
            cols = slice(t * P, (t + 1) * P)
            quantize(w1_codes[:, cols], w1_scales[:, cols], w1_g[:, t * N : (t + 1) * N])
            product(a_bank[t][:], w1_codes, w1_scales, t, xa_words[:], xa_scales[:])

        w2_g = sb("w2_g", [P, PACK * N], BF16)
        w2_codes = sb("w2_codes", [P, N], U32)
        w2_scales = sb("w2_scales", [P, N], U8)
        b_bank = [psum.tile([P, N], F32, name="b_bank%d" % t, tag="bank%d" % (PACK + t)) for t in range(PACK)]
        sig = [sb("sig%d" % t, [P, UPDATED], F32) for t in range(PACK)]
        upd = [sb("upd%d" % t, [P, UPDATED], F32) for t in range(PACK)]
        z_planes = sb("z_planes", [P, PACK, N], BF16)

        def a_out(t):
            nc.vector.tensor_scalar(a_win[t][:, :N], a_bank[t][:], 0.5, None, ALU.mult)

        def a_sigmoid(t):
            nc.scalar.activation(sig[t][:], a_win[t][:].indirect(n2_t[:]), ACT.Sigmoid, scale=-4.0)

        def a_add(t):
            nc.vector.tensor_tensor(upd[t][:], a_win[t][:].indirect(n1_t[:]), sig[t][:], ALU.add)

        def a_put(t):
            nc.scalar.activation(a_win[t][:].indirect(n1_t[:]), upd[t][:], ACT.Copy, bias=-0.5)

        a_out(0)
        a_out(1)
        a_sigmoid(0)
        a_sigmoid(1)
        a_add(0)
        a_put(0)
        a_out(2)
        deal_weights(nc.vector.tensor_copy, w2_raw, w2_g, 0, P)
        a_out(3)
        a_sigmoid(2)
        a_sigmoid(3)
        a_add(1)
        quantize(w2_codes[:], w2_scales[:], w2_g[:])
        for t in range(PACK):
            product(b_bank[t][:], w2_codes, w2_scales, t, xb_words[:], xb_scales[:])
        a_add(2)
        a_add(3)
        for t in range(1, PACK):
            a_put(t)

        z_g = sb("z_g", [P, PACK * N], BF16)
        z_codes = sb("z_codes", [P, N], U32)
        z_scales = sb("z_scales", [P, N], U8)
        b_win = [sb("b_win%d" % t, [P, N], F32) for t in range(PACK)]
        z2_codes = sb("z2_codes", [P, N], U32)
        z2_scales = sb("z2_scales", [P, N], U8)
        z2_planes = [sb("z2_planes%d" % k, [P, PACK, hi - lo], BF16) for k, (lo, hi) in enumerate(Z2_PARTS)]
        z2_g = [sb("z2_g%d" % k, [P, PACK * (hi - lo)], BF16) for k, (lo, hi) in enumerate(Z2_PARTS)]
        at_n3 = [sb("at_n3_%d" % t, [P, N], F32) for t in range(PACK)]
        at_n4 = [sb("at_n4_%d" % t, [P, N], F32) for t in range(PACK)]

        def fetch_scalar(dst, src):
            nc.scalar.activation(dst, src, ACT.Copy)

        def b_at(t, picks, lo, hi):
            return b_win[t][:].indirect(picks[:, lo // 16 : hi // 16])

        for t in VECTOR_PLANES:
            nc.vector.tensor_copy(b_win[t][:], b_bank[t][:])
        for t in SCALAR_PLANES:
            nc.scalar.copy(b_win[t][:], b_bank[t][:])
        for lo, hi in Z2_PARTS:
            for t in SCALAR_PLANES:
                fetch_scalar(at_n3[t][:, lo:hi], b_at(t, n3_t, lo, hi))
                fetch_scalar(at_n4[t][:, lo:hi], b_at(t, n4_t, lo, hi))
        for lo, hi in ((0, N // 2), (N // 2, N)):
            for t in VECTOR_PLANES:
                nc.vector.tensor_copy(at_n3[t][:, lo:hi], b_at(t, n3_t, lo, hi))
            for t in VECTOR_PLANES:
                nc.vector.tensor_tensor(at_n4[t][:, lo:hi], b_at(t, n4_t, lo, hi), at_n3[t][:, lo:hi], ALU.mult)

        for k, (lo, hi) in enumerate(Z2_PARTS):
            for t in VECTOR_PLANES:
                nc.vector.tensor_scalar(z2_planes[k][:, t, :], at_n4[t][:, lo:hi], gb_t[:, t : t + 1], None, ALU.mult)
        for t in range(PACK):
            nc.vector.tensor_scalar(z_planes[:, t, :], a_win[t][:, :N], ga_t[:, t : t + 1], 2.0, ALU.mult, ALU.mult)

        def z2_times(k, t):
            lo, hi = Z2_PARTS[k]
            nc.vector.scalar_tensor_tensor(
                z2_planes[k][:, t, :], at_n3[t][:, lo:hi], gb_t[:, t : t + 1], at_n4[t][:, lo:hi], ALU.mult, ALU.mult
            )

        def weave(grouped, planes):
            nc.vector.tensor_copy(
                grouped[:].rearrange("p (c i t) -> p c t i", i=4, t=PACK),
                planes[:].rearrange("p t (c i) -> p c t i", i=4),
            )

        s_bank = [
            [
                psum.tile([P, hi - lo], F32, name="s_bank%d_%d" % (k, i), tag="bank%d" % (PACK * (k % 2) + i))
                for i in range(PACK)
            ]
            for k, (lo, hi) in enumerate(Z2_PARTS)
        ]

        def s_products(k):
            cols = slice(*Z2_PARTS[k])
            quantize(z2_codes[:, cols], z2_scales[:, cols], z2_g[k][:])
            for i in range(PACK):
                product(s_bank[k][i][:], z_codes, z_scales, i, z2_codes[:, cols], z2_scales[:, cols])

        def s_out(k, i):
            nc.scalar.activation(s_win[i][:, slice(*Z2_PARTS[k])], s_bank[k][i][:], ACT.Copy, scale=0.0625)

        first, second = SCALAR_PLANES
        z2_times(0, first)
        weave(z_g, z_planes)
        z2_times(0, second)
        quantize(z_codes[:], z_scales[:], z_g[:])
        weave(z2_g[0], z2_planes[0])
        z2_times(1, first)
        s_products(0)
        z2_times(1, second)
        z2_times(2, first)
        for i in range(PACK):
            s_out(0, i)
        weave(z2_g[1], z2_planes[1])
        z2_times(2, second)
        s_products(1)
        for i in range(PACK):
            s_out(1, i)
        weave(z2_g[2], z2_planes[2])
        s_products(2)

        mb = [sb("mb%d" % i, [P, MEMBERS * N], F32) for i in range(PACK)]
        pair = [sb("pair%d" % i, [P, 2 * N], F32) for i in range(PACK)]
        top = [sb("top%d" % i, [P, N], F32) for i in range(PACK)]
        res = [sb("res%d" % i, [P, N], F32) for i in range(PACK)]

        def members(fetch, i, lo, hi):
            entries = slice(MEMBERS * lo // 16, MEMBERS * hi // 16)
            fetch(mb[i][:, MEMBERS * lo : MEMBERS * hi], s_win[i][:].indirect(n5_t[:, entries]))

        def max_pairs(i, lo, hi):
            four = mb[i][:, MEMBERS * lo : MEMBERS * hi].rearrange("p (v a b) -> p v a b", a=2, b=2)
            both = pair[i][:, 2 * lo : 2 * hi].rearrange("p (v b) -> p v b", b=2)
            nc.vector.tensor_tensor(both, four[:, :, 0, :], four[:, :, 1, :], ALU.max)

        def max_top(i, lo, hi):
            both = pair[i][:, 2 * lo : 2 * hi].rearrange("p (v b) -> p v b", b=2)
            nc.vector.tensor_tensor(top[i][:, lo:hi], both[:, :, 0], both[:, :, 1], ALU.max)

        def finish(i, lo, hi):
            nc.vector.tensor_tensor(res[i][:, lo:hi], s_win[i][:, lo:hi], top[i][:, lo:hi], ALU.subtract)
            nc.sync.dma_start(out[i * P : (i + 1) * P, lo:hi], res[i][:, lo:hi])

        last = PACK - 1
        for i in range(last):
            s_out(2, i)
        for i in range(last):
            members(fetch_scalar, i, EVEN_CUTS[0], EVEN_CUTS[1])
            members(fetch_scalar, i, EVEN_CUTS[1], EVEN_CUTS[2])
            if i == 0:
                s_out(2, last)
        for k in range(3):
            members(fetch_scalar, last, LAST_CUTS[k], LAST_CUTS[k + 1])

        for i in range(last):
            members(nc.vector.tensor_copy, i, 0, VECTOR_COLS)
        max_pairs(0, 0, N)
        members(nc.vector.tensor_copy, last, 0, VECTOR_COLS // 2)
        max_top(0, 0, N)
        members(nc.vector.tensor_copy, last, VECTOR_COLS // 2, VECTOR_COLS)
        finish(0, 0, N)
        for step in (max_pairs, max_top, finish):
            step(1, 0, N)
            step(last, 0, LAST_CUTS[0])
        for step in (max_pairs, max_top, finish):
            step(2, 0, N)
            step(last, LAST_CUTS[0], LAST_CUTS[1])
        max_pairs(last, LAST_CUTS[1], LAST_CUTS[2])
        max_top(last, LAST_CUTS[1], LAST_CUTS[2])
        nc.vector.tensor_reduce(
            top[last][:, LAST_CUTS[2] :],
            mb[last][:, MEMBERS * LAST_CUTS[2] :].rearrange("p (v a) -> p v a", a=MEMBERS),
            mybir.AxisListType.X,
            ALU.max,
        )
        finish(last, LAST_CUTS[1], LAST_CUTS[2])
        finish(last, LAST_CUTS[2], LAST_CUTS[3])
